import numpy as np
import ml_dtypes


def mxq(x, axis, fmt="e4m3"):
    dtype, down = {"e4m3": (ml_dtypes.float8_e4m3fn, 7), "e5m2": (ml_dtypes.float8_e5m2, 14)}[fmt]
    v = np.moveaxis(np.asarray(x, np.float32).astype(ml_dtypes.bfloat16).astype(np.float64), axis, -1)
    blocks = v.reshape(v.shape[:-1] + (-1, 32))
    amax = np.abs(blocks).max(-1, keepdims=True)
    byte = np.maximum(np.where(amax > 0, np.frexp(amax)[1] - 1 + 127, 0) - down, 1)
    scale = np.exp2(byte - 127.0)
    codes = (blocks / scale).astype(np.float32).astype(dtype).astype(np.float64)
    return np.moveaxis((codes * scale).reshape(v.shape), -1, axis)


WIDE = False


def mx_kscale(k):
    if not WIDE:
        return np.ones(k)
    levels = np.array([10, -10, 5, -5, 0])
    if k % 512:
        return np.exp2(np.random.permutation(np.resize(levels, k // 32))).repeat(32)
    a = np.empty((k // 512, 16))
    for p in range(k // 512):
        a[p, :8] = np.random.permutation(np.resize(levels, 8))
        for g in range(8):
            far = levels[np.abs(levels - a[p, g]) >= 10]
            a[p, g + 8] = far[np.random.randint(len(far))]
    return np.exp2(a.ravel()).repeat(32)


def f64(x):
    return np.asarray(x).astype(np.float64)


def striped(idx):
    return np.tile(idx.reshape(-1, 16).T, (8, 1)).astype(np.uint16)


def unstriped(offs):
    return offs[:16].T.reshape(-1).astype(np.int64)


def striped8(idx):
    return np.concatenate([x.reshape(-1, 16).T for x in idx]).astype(np.uint16)


def runs(offs, k):
    lists = np.stack([offs[16 * r : 16 * r + 16].T.reshape(-1) for r in range(8)]).astype(np.int64)
    return lists[np.arange(k) % 512 // 64]


def pack_weight(w):
    k, n = w.shape
    w = f64(np.asarray(w, np.float32).astype(ml_dtypes.bfloat16)).reshape(k // 32, 32, n)
    amax = np.abs(w).max(1)
    byte = np.clip(np.where(amax > 0, np.frexp(amax)[1] - 1 + 127 - 7, 1), 1, 254)
    scaled = (w * np.exp2(127.0 - byte)[:, None, :]).reshape(k, n).astype(np.float32)
    words = np.ascontiguousarray(scaled.reshape(k // 512, 128, 4, n).transpose(0, 1, 3, 2)).astype(ml_dtypes.float8_e4m3fn).view(np.uint8)
    return words, np.ascontiguousarray(byte.astype(np.uint8).reshape(k // 512, 16, n))


def unpack_weight(words, scales):
    g, p, n, _ = words.shape
    vals = np.ascontiguousarray(words).view(ml_dtypes.float8_e4m3fn).astype(np.float64) * np.repeat(np.exp2(scales.astype(np.float64) - 127.0), 8, axis=1)[..., None]
    return vals.transpose(0, 1, 3, 2).reshape(g * 512, n)


E2M1 = np.array([0.0, 0.5, 1.0, 1.5, 2.0, 3.0, 4.0, 6.0, -0.0, -0.5, -1.0, -1.5, -2.0, -3.0, -4.0, -6.0])


def pack_fp4(w):
    k, n = w.shape
    w = f64(np.asarray(w, np.float32).astype(ml_dtypes.bfloat16)).reshape(k // 32, 32, n)
    amax = np.abs(w).max(1)
    mant, ex = np.frexp(amax / 6.0)
    byte = np.clip(np.where(amax > 0, np.where(mant > 0.5, ex, ex - 1) + 127, 1), 1, 254)
    scaled = (w * np.exp2(127.0 - byte)[:, None, :]).reshape(k, n).astype(np.float32)
    c = np.ascontiguousarray(scaled.reshape(k // 512, 128, 4, n).transpose(0, 1, 3, 2)).astype(ml_dtypes.float4_e2m1fn).view(np.uint8) & 0xF
    words = (c[..., 0::2] | (c[..., 1::2] << 4)).reshape(k // 512, 128, 2 * n)
    return np.ascontiguousarray(words), np.ascontiguousarray(byte.astype(np.uint8).reshape(k // 512, 16, n))


def unpack_fp4(words, scales):
    g, _, n = scales.shape
    words = np.ascontiguousarray(words).reshape(g, 128, n, 2)
    nib = np.empty((g, 128, n, 4), np.uint8)
    nib[..., 0::2] = words & 0xF
    nib[..., 1::2] = words >> 4
    vals = E2M1[nib] * np.repeat(np.exp2(scales.astype(np.float64) - 127.0), 8, axis=1)[..., None]
    return vals.transpose(0, 1, 3, 2).reshape(g * 512, n)


def sigmoid(v):
    return 1.0 / (1.0 + np.exp(-np.maximum(v, -700.0)))


K, T, S, N, G, H, U = 512, 2048, 256, 512, 2048, 512, 512


def setup_inputs():
    n = np.random.standard_normal
    s = mx_kscale(K)[:, None]
    u = mx_kscale(K)
    packed_xT = pack_weight(n((K, T)) * s)
    packed_dT = pack_weight(n((K, G)) / s)
    packed_w1 = pack_fp4(n((H, N)) / np.sqrt(H) / u[:, None])
    perm = np.random.permutation(U)
    return {
        "x_words": packed_xT[0],
        "x_scales": packed_xT[1],
        "d_words": packed_dT[0],
        "d_scales": packed_dT[1],
        "sl": np.random.uniform(1.0, 2.0, (H, 1)).astype(np.float32),
        "th": (0.5 * n((H, 1))).astype(np.float32),
        "gn": (np.random.uniform(0.5, 1.5, (H, 1)) * u[:, None]).astype(np.float32),
        "w1_words": packed_w1[0],
        "w1_scales": packed_w1[1],
        "offs": striped8(np.random.randint(0, T, (8, S))),
        "ci": striped(np.random.permutation(G)[:H]),
        "n1": striped8(np.stack([np.random.permutation(S) for _ in range(8)])),
        "n2": striped(perm[:S]),
        "n3": striped(perm[S:]),
        "n4": striped(np.random.permutation(U)),
    }


def reference(x_words, x_scales, d_words, d_scales, sl, th, gn, w1_words, w1_scales, offs, ci, n1, n2, n3, n4):
    d_ci = unpack_weight(d_words, d_scales)[:, unstriped(ci)]
    xq = unpack_weight(x_words, x_scales)[np.arange(K)[:, None], runs(offs, K)]
    s = 0.0625 * (d_ci.T @ xq)
    sg = sigmoid(f64(sl) * (s[np.arange(H)[:, None], runs(n1, H)] - f64(th)))
    z = f64(gn) * (s * sg)
    h = unpack_fp4(w1_words, w1_scales).T @ mxq(z, 0, "e4m3")
    nw = 0.5 * h
    ph = np.zeros((N, U))
    ph[:, unstriped(n2)] = h
    pg = ph.copy()
    pg[:, unstriped(n3)] = nw
    return pg - pg[:, unstriped(n4)]

@@ -1,0 +1,155 @@
+from contextlib import ExitStack
+
+import concourse.mybir as mybir
+
+F32 = mybir.dt.float32
+BF16 = mybir.dt.bfloat16
+I32 = mybir.dt.int32
+U32 = mybir.dt.uint32
+U16 = mybir.dt.uint16
+U8 = mybir.dt.uint8
+FP8X4 = mybir.dt.float8_e4m3fn_x4
+FP4X4 = mybir.dt.float4_e2m1fn_x4
+ACT = mybir.ActivationFunctionType
+ALU = mybir.AluOpType
+
+P = 128
+PACK = 4
+K, T, S, H, N, U = 512, 2048, 256, 512, 512, 512
+HALF = S // 2
+FLOPS = 2 * K * H * S + 2 * H * N * S
+
+
+def entries(lst, a, b):
+    return lst[:, a // 16 : b // 16]
+
+
+def tile_picked_hwlesapagtwo_none_p_kernel(
+    tc, x_words, x_scales, d_words, d_scales, sl, th, gn, w1_words, w1_scales, offs, ci, n1, n2, n3, n4, out
+):
+    nc = tc.nc
+    with ExitStack() as ctx:
+        lists = ctx.enter_context(tc.tile_pool(name="lists", bufs=1))
+        keep = ctx.enter_context(tc.tile_pool(name="keep", bufs=1))
+        psum = ctx.enter_context(tc.psum_pool(name="psum", bufs=1))
+
+        def load_list(src, name):
+            tile = lists.tile([P, src.shape[1]], U16, name=name)
+            nc.sync.dma_start(tile[:], src)
+            return tile
+
+        x_bytes = keep.tile([P, T], U8, name="x_bytes")
+        d_bytes = keep.tile([P, T], U8, name="d_bytes")
+        plane1 = keep.tile([P, S + H], U8, name="plane1", align_bytes=64)
+        w_plane = keep.tile([P, N], U8, name="w_plane", align_bytes=64)
+        for tile in (x_bytes, d_bytes, plane1, w_plane):
+            nc.vector.memset(tile[:].bitcast(I32), 0)
+
+        x_table = keep.tile([P, T], U32, name="x_table")
+        d_table = keep.tile([P, T], U32, name="d_table")
+        w_codes = keep.tile([P, 2 * N], U8, name="w_codes", align_bytes=64)
+        offs_t = load_list(offs, "offs_t")
+        ci_t = load_list(ci, "ci_t")
+        n1_t = load_list(n1, "n1_t")
+        nc.scalar.dma_start(x_bytes[0:P:8, :].bitcast(I32), x_scales[0].bitcast(I32))
+        nc.scalar.dma_start(d_bytes[0:P:8, :].bitcast(I32), d_scales[0].bitcast(I32))
+        nc.sync.dma_start(d_table[:].bitcast(I32), d_words[0].rearrange("p c r -> p (c r)").bitcast(I32))
+        n2_t = load_list(n2, "n2_t")
+        n3_t = load_list(n3, "n3_t")
+        n4_t = load_list(n4, "n4_t")
+        nc.sync.dma_start(x_table[:].bitcast(I32), x_words[0].rearrange("p c r -> p (c r)").bitcast(I32))
+        nc.sync.dma_start(w_codes[:].bitcast(I32), w1_words[0].bitcast(I32))
+
+        sl_t = keep.tile([P, PACK], F32, name="sl_t")
+        th_t = keep.tile([P, PACK], F32, name="th_t")
+        gn_t = keep.tile([P, PACK], F32, name="gn_t")
+        for tile, src in ((sl_t, sl), (th_t, th), (gn_t, gn)):
+            nc.gpsimd.dma_start(tile[:], src.rearrange("(p t) o -> p (t o)", t=PACK))
+        for q in range(4):
+            nc.gpsimd.dma_start(w_plane[32 * q : 32 * q + 4, :].bitcast(I32), w1_scales[0, 4 * q : 4 * q + 4, :].bitcast(I32))
+
+        picked_bytes = keep.tile([P, S + H], U8, name="picked_bytes")
+        nc.vector.tensor_copy(picked_bytes[:, 0:S], x_bytes[:].indirect(offs_t[:]))
+        nc.vector.tensor_copy(picked_bytes[:, S : S + H].rearrange("p (t m) -> p m t", t=PACK), d_bytes[:].indirect(ci_t[:]))
+        for k in range(4):
+            nc.scalar.dma_start(plane1[k:P:32, :].bitcast(I32), picked_bytes[8 * k : P : 32, :].bitcast(I32))
+
+        d_codes = keep.tile([P, H], U32, name="d_codes", align_bytes=64)
+        x_codes = keep.tile([P, S], U32, name="x_codes", align_bytes=64)
+        nc.vector.tensor_copy(d_codes[:].rearrange("p (t m) -> p m t", t=PACK), d_table[:].indirect(ci_t[:]))
+        bias_t = keep.tile([P, PACK], F32, name="bias_t")
+        nc.vector.scalar_tensor_tensor(bias_t[:], sl_t[:], -1.0, th_t[:], ALU.mult, ALU.mult)
+        nc.vector.tensor_copy(x_codes[:], x_table[:].indirect(offs_t[:]))
+
+        s_rows = []
+        for t in range(PACK):
+            acc = psum.tile([P, S], F32, name="s_acc%d" % t)
+            nc.tensor.matmul_mx(
+                out=acc[:],
+                lhsT=d_codes[:, t * P : (t + 1) * P].bitcast(FP8X4),
+                lhsT_scale=plane1[:, S + t * P : S + (t + 1) * P],
+                rhs=x_codes[:].bitcast(FP8X4),
+                rhs_scale=plane1[:, 0:S],
+                start=True,
+                stop=True,
+            )
+            s_t = keep.tile([P, S], F32, name="s%d" % t)
+            nc.vector.tensor_scalar(s_t[:], acc[:], 0.0625, None, ALU.mult)
+            s_rows.append(s_t)
+
+        h_all = keep.tile([P, N // P, S], F32, name="h_all")
+        for half in range(2):
+            c0, c1 = half * HALF, (half + 1) * HALF
+            sg = keep.tile([P, PACK, HALF], F32, name="sg%d" % half)
+            z = keep.tile([P, PACK, HALF], BF16, name="z")
+            for t in range(PACK):
+                nc.scalar.activation(
+                    sg[:, t, :], s_rows[t][:].indirect(entries(n1_t, c0, c1)), ACT.Sigmoid,
+                    bias=bias_t[:, t : t + 1], scale=sl_t[:, t : t + 1],
+                )
+                nc.vector.scalar_tensor_tensor(
+                    z[:, t, :], s_rows[t][:, c0:c1], gn_t[:, t : t + 1], sg[:, t, :], ALU.mult, ALU.mult
+                )
+            z_in = keep.tile([P, HALF, PACK], BF16, name="z_in%d" % half, align_bytes=64)
+            nc.vector.tensor_copy(
+                z_in[:].rearrange("p (c i) t -> p c t i", i=4), z[:].rearrange("p t (c i) -> p c t i", i=4)
+            )
+            z_codes = keep.tile([P, HALF], U32, name="z_codes%d" % half, align_bytes=64)
+            z_plane = keep.tile([P, HALF], U8, name="z_plane%d" % half, align_bytes=64)
+            nc.vector.quantize_mx(z_codes[:].bitcast(FP8X4), z_plane[:], z_in[:].rearrange("p j t -> p (j t)"))
+            for m0, m1 in ((0, 1), (1, 4)):
+                acc = psum.tile([P, m1 - m0, HALF], F32, name="h_acc%d_%d" % (half, m0))
+                for m in range(m0, m1):
+                    nc.tensor.matmul_mx(
+                        out=acc[:, m - m0, :],
+                        lhsT=w_codes[:, 2 * m * P : 2 * (m + 1) * P].bitcast(FP4X4),
+                        lhsT_scale=w_plane[:, m * P : (m + 1) * P],
+                        rhs=z_codes[:].bitcast(FP8X4),
+                        rhs_scale=z_plane[:],
+                        start=True,
+                        stop=True,
+                    )
+                nc.vector.tensor_copy(h_all[:, m0:m1, c0:c1], acc[:])
+
+        pages = [keep.tile([P, U], F32, name="page%d" % m) for m in range(N // P)]
+
+        def put(m, lst, factor, c0, c1):
+            nc.scalar.activation(pages[m][:].indirect(entries(lst, c0, c1)), h_all[:, m, c0:c1], ACT.Copy, scale=factor)
+
+        def take(m, w0, w1):
+            other = keep.tile([P, w1 - w0], F32, name="other%d_%d" % (m, w0))
+            nc.scalar.activation(other[:], pages[m][:].indirect(entries(n4_t, w0, w1)), ACT.Copy)
+            res = keep.tile([P, w1 - w0], F32, name="res%d_%d" % (m, w0))
+            nc.vector.tensor_tensor(res[:], pages[m][:, w0:w1], other[:], ALU.subtract)
+            nc.sync.dma_start(out[m * P : (m + 1) * P, w0:w1], res[:])
+
+        for c0 in (0, HALF):
+            put(0, n2_t, 1.0, c0, c0 + HALF)
+            put(0, n3_t, 0.5, c0, c0 + HALF)
+        for m in range(1, N // P):
+            put(m, n2_t, 1.0, 0, S)
+            take(m - 1, 0, U // 2)
+            put(m, n3_t, 0.5, 0, S)
+            take(m - 1, U // 2, U)
+        take(N // P - 1, 0, U // 2)
+        take(N // P - 1, U // 2, U)

@@ -39,25 +39,26 @@ def tile_picked_hwlesapagtwo_none_p_kernel(
             return tile
 
         x_bytes = keep.tile([P, T], U8, name="x_bytes")
-        d_bytes = keep.tile([P, T], U8, name="d_bytes")
+        d_bytes = keep.tile([P, T], U8, name="d_bytes", tag="d_bytes_then_w_plane", align_bytes=64)
         plane1 = keep.tile([P, S + H], U8, name="plane1", align_bytes=64)
-        w_plane = keep.tile([P, N], U8, name="w_plane", align_bytes=64)
-        for tile in (x_bytes, d_bytes, plane1, w_plane):
-            nc.vector.memset(tile[:].bitcast(I32), 0)
+        nc.vector.memset(plane1[:].bitcast(I32), 0)
+
+        def block_rows(scales):
+            return scales[0].bitcast(I32).unsqueeze(1).to_broadcast([16, 8, T // 4])
 
         x_table = keep.tile([P, T], U32, name="x_table")
-        d_table = keep.tile([P, T], U32, name="d_table")
+        d_table = keep.tile([P, T], U32, name="d_table", tag="d_table_then_bias")
         w_codes = keep.tile([P, 2 * N], U8, name="w_codes", align_bytes=64)
         offs_t = load_list(offs, "offs_t")
+        nc.sync.dma_start(x_bytes[:].bitcast(I32), block_rows(x_scales))
         ci_t = load_list(ci, "ci_t")
-        n1_t = load_list(n1, "n1_t")
-        nc.scalar.dma_start(x_bytes[0:P:8, :].bitcast(I32), x_scales[0].bitcast(I32))
-        nc.scalar.dma_start(d_bytes[0:P:8, :].bitcast(I32), d_scales[0].bitcast(I32))
+        nc.sync.dma_start(d_bytes[:].bitcast(I32), block_rows(d_scales))
         nc.sync.dma_start(d_table[:].bitcast(I32), d_words[0].rearrange("p c r -> p (c r)").bitcast(I32))
+        n1_t = load_list(n1, "n1_t")
         n2_t = load_list(n2, "n2_t")
         n3_t = load_list(n3, "n3_t")
-        n4_t = load_list(n4, "n4_t")
         nc.sync.dma_start(x_table[:].bitcast(I32), x_words[0].rearrange("p c r -> p (c r)").bitcast(I32))
+        n4_t = load_list(n4, "n4_t")
         nc.sync.dma_start(w_codes[:].bitcast(I32), w1_words[0].bitcast(I32))
 
         sl_t = keep.tile([P, PACK], F32, name="sl_t")
@@ -65,8 +66,6 @@ def tile_picked_hwlesapagtwo_none_p_kernel(
         gn_t = keep.tile([P, PACK], F32, name="gn_t")
         for tile, src in ((sl_t, sl), (th_t, th), (gn_t, gn)):
             nc.gpsimd.dma_start(tile[:], src.rearrange("(p t) o -> p (t o)", t=PACK))
-        for q in range(4):
-            nc.gpsimd.dma_start(w_plane[32 * q : 32 * q + 4, :].bitcast(I32), w1_scales[0, 4 * q : 4 * q + 4, :].bitcast(I32))
 
         picked_bytes = keep.tile([P, S + H], U8, name="picked_bytes")
         nc.vector.tensor_copy(picked_bytes[:, 0:S], x_bytes[:].indirect(offs_t[:]))
@@ -74,10 +73,15 @@ def tile_picked_hwlesapagtwo_none_p_kernel(
         for k in range(4):
             nc.scalar.dma_start(plane1[k:P:32, :].bitcast(I32), picked_bytes[8 * k : P : 32, :].bitcast(I32))
 
+        w_plane = keep.tile([P, N], U8, name="w_plane", tag="d_bytes_then_w_plane", align_bytes=64)
+        nc.vector.memset(w_plane[:].bitcast(I32), 0)
+        for q in range(4):
+            nc.sync.dma_start(w_plane[32 * q : 32 * q + 4, :].bitcast(I32), w1_scales[0, 4 * q : 4 * q + 4, :].bitcast(I32))
+
         d_codes = keep.tile([P, H], U32, name="d_codes", align_bytes=64)
         x_codes = keep.tile([P, S], U32, name="x_codes", align_bytes=64)
         nc.vector.tensor_copy(d_codes[:].rearrange("p (t m) -> p m t", t=PACK), d_table[:].indirect(ci_t[:]))
-        bias_t = keep.tile([P, PACK], F32, name="bias_t")
+        bias_t = keep.tile([P, PACK], F32, name="bias_t", tag="d_table_then_bias")
         nc.vector.scalar_tensor_tensor(bias_t[:], sl_t[:], -1.0, th_t[:], ALU.mult, ALU.mult)
         nc.vector.tensor_copy(x_codes[:], x_table[:].indirect(offs_t[:]))
 
@@ -117,7 +121,7 @@ def tile_picked_hwlesapagtwo_none_p_kernel(
             z_codes = keep.tile([P, HALF], U32, name="z_codes%d" % half, align_bytes=64)
             z_plane = keep.tile([P, HALF], U8, name="z_plane%d" % half, align_bytes=64)
             nc.vector.quantize_mx(z_codes[:].bitcast(FP8X4), z_plane[:], z_in[:].rearrange("p j t -> p (j t)"))
-            for m0, m1 in ((0, 1), (1, 4)):
+            for m0, m1 in ((0, 1), (1, 4)) if half == 0 else ((0, 4),):
                 acc = psum.tile([P, m1 - m0, HALF], F32, name="h_acc%d_%d" % (half, m0))
                 for m in range(m0, m1):
                     nc.tensor.matmul_mx(
@@ -129,7 +133,10 @@ def tile_picked_hwlesapagtwo_none_p_kernel(
                         start=True,
                         stop=True,
                     )
-                nc.vector.tensor_copy(h_all[:, m0:m1, c0:c1], acc[:])
+                if m1 == 1:
+                    nc.scalar.copy(h_all[:, m0:m1, c0:c1], acc[:])
+                else:
+                    nc.vector.tensor_copy(h_all[:, m0:m1, c0:c1], acc[:])
 
         pages = [keep.tile([P, U], F32, name="page%d" % m) for m in range(N // P)]
 
@@ -143,13 +150,12 @@ def tile_picked_hwlesapagtwo_none_p_kernel(
             nc.vector.tensor_tensor(res[:], pages[m][:, w0:w1], other[:], ALU.subtract)
             nc.sync.dma_start(out[m * P : (m + 1) * P, w0:w1], res[:])
 
-        for c0 in (0, HALF):
-            put(0, n2_t, 1.0, c0, c0 + HALF)
-            put(0, n3_t, 0.5, c0, c0 + HALF)
-        for m in range(1, N // P):
-            put(m, n2_t, 1.0, 0, S)
-            take(m - 1, 0, U // 2)
-            put(m, n3_t, 0.5, 0, S)
-            take(m - 1, U // 2, U)
-        take(N // P - 1, 0, U // 2)
-        take(N // P - 1, U // 2, U)
+        for pair in ((0, 1), (2, 3)):
+            for c0, c1 in ((0, HALF), (HALF, S)) if pair[0] == 0 else ((0, S),):
+                for lst, factor in ((n2_t, 1.0), (n3_t, 0.5)):
+                    for m in pair:
+                        put(m, lst, factor, c0, c1)
+            for m in pair:
+                cuts = (0, 256, 448, U) if m == N // P - 1 else (0, 256, U)
+                for w0, w1 in zip(cuts, cuts[1:]):
+                    take(m, w0, w1)

@@ -31,6 +31,7 @@ def tile_picked_hwlesapagtwo_none_p_kernel(
     with ExitStack() as ctx:
         lists = ctx.enter_context(tc.tile_pool(name="lists", bufs=1))
         keep = ctx.enter_context(tc.tile_pool(name="keep", bufs=1))
+        reuse = ctx.enter_context(tc.tile_pool(name="reuse", bufs=1))
         psum = ctx.enter_context(tc.psum_pool(name="psum", bufs=1))
 
         def load_list(src, name):
@@ -39,27 +40,23 @@ def tile_picked_hwlesapagtwo_none_p_kernel(
             return tile
 
         x_bytes = keep.tile([P, T], U8, name="x_bytes")
-        d_bytes = keep.tile([P, T], U8, name="d_bytes", tag="d_bytes_then_w_plane", align_bytes=64)
+        d_bytes = keep.tile([P, T], U8, name="d_bytes")
         plane1 = keep.tile([P, S + H], U8, name="plane1", align_bytes=64)
-        nc.vector.memset(plane1[:].bitcast(I32), 0)
-
-        def block_rows(scales):
-            return scales[0].bitcast(I32).unsqueeze(1).to_broadcast([16, 8, T // 4])
+        for tile in (x_bytes, d_bytes, plane1):
+            nc.vector.memset(tile[:].bitcast(I32), 0)
 
         x_table = keep.tile([P, T], U32, name="x_table")
-        d_table = keep.tile([P, T], U32, name="d_table", tag="d_table_then_bias")
-        w_codes = keep.tile([P, 2 * N], U8, name="w_codes", align_bytes=64)
+        d_table = reuse.tile([P, T], U32, name="d_table", offset=0, align_bytes=64)
         offs_t = load_list(offs, "offs_t")
-        nc.sync.dma_start(x_bytes[:].bitcast(I32), block_rows(x_scales))
         ci_t = load_list(ci, "ci_t")
-        nc.sync.dma_start(d_bytes[:].bitcast(I32), block_rows(d_scales))
-        nc.sync.dma_start(d_table[:].bitcast(I32), d_words[0].rearrange("p c r -> p (c r)").bitcast(I32))
         n1_t = load_list(n1, "n1_t")
         n2_t = load_list(n2, "n2_t")
         n3_t = load_list(n3, "n3_t")
-        nc.sync.dma_start(x_table[:].bitcast(I32), x_words[0].rearrange("p c r -> p (c r)").bitcast(I32))
+        nc.sync.dma_start(x_bytes[0:P:8, :].bitcast(I32), x_scales[0].bitcast(I32))
+        nc.sync.dma_start(d_bytes[0:P:8, :].bitcast(I32), d_scales[0].bitcast(I32))
+        nc.sync.dma_start(d_table[:].bitcast(I32), d_words[0].rearrange("p c r -> p (c r)").bitcast(I32))
         n4_t = load_list(n4, "n4_t")
-        nc.sync.dma_start(w_codes[:].bitcast(I32), w1_words[0].bitcast(I32))
+        nc.sync.dma_start(x_table[:].bitcast(I32), x_words[0].rearrange("p c r -> p (c r)").bitcast(I32))
 
         sl_t = keep.tile([P, PACK], F32, name="sl_t")
         th_t = keep.tile([P, PACK], F32, name="th_t")
@@ -73,15 +70,16 @@ def tile_picked_hwlesapagtwo_none_p_kernel(
         for k in range(4):
             nc.scalar.dma_start(plane1[k:P:32, :].bitcast(I32), picked_bytes[8 * k : P : 32, :].bitcast(I32))
 
-        w_plane = keep.tile([P, N], U8, name="w_plane", tag="d_bytes_then_w_plane", align_bytes=64)
-        nc.vector.memset(w_plane[:].bitcast(I32), 0)
-        for q in range(4):
-            nc.sync.dma_start(w_plane[32 * q : 32 * q + 4, :].bitcast(I32), w1_scales[0, 4 * q : 4 * q + 4, :].bitcast(I32))
-
         d_codes = keep.tile([P, H], U32, name="d_codes", align_bytes=64)
         x_codes = keep.tile([P, S], U32, name="x_codes", align_bytes=64)
         nc.vector.tensor_copy(d_codes[:].rearrange("p (t m) -> p m t", t=PACK), d_table[:].indirect(ci_t[:]))
-        bias_t = keep.tile([P, PACK], F32, name="bias_t", tag="d_table_then_bias")
+        w_codes = reuse.tile([P, 2 * N], U8, name="w_codes", offset=0, align_bytes=64)
+        w_plane = reuse.tile([P, N], U8, name="w_plane", offset=2 * N, align_bytes=64)
+        bias_t = reuse.tile([P, PACK], F32, name="bias_t", offset=3 * N, align_bytes=64)
+        nc.vector.memset(w_plane[:].bitcast(I32), 0)
+        nc.sync.dma_start(w_codes[:].bitcast(I32), w1_words[0].bitcast(I32))
+        for q in range(4):
+            nc.sync.dma_start(w_plane[32 * q : 32 * q + 4, :].bitcast(I32), w1_scales[0, 4 * q : 4 * q + 4, :].bitcast(I32))
         nc.vector.scalar_tensor_tensor(bias_t[:], sl_t[:], -1.0, th_t[:], ALU.mult, ALU.mult)
         nc.vector.tensor_copy(x_codes[:], x_table[:].indirect(offs_t[:]))
 

from contextlib import ExitStack

import concourse.mybir as mybir

F32 = mybir.dt.float32
BF16 = mybir.dt.bfloat16
I32 = mybir.dt.int32
U32 = mybir.dt.uint32
U16 = mybir.dt.uint16
U8 = mybir.dt.uint8
FP8X4 = mybir.dt.float8_e4m3fn_x4
FP4X4 = mybir.dt.float4_e2m1fn_x4
ACT = mybir.ActivationFunctionType
ALU = mybir.AluOpType

P = 128
PACK = 4
K, T, S, H, N, U = 512, 2048, 256, 512, 512, 512
HALF = S // 2
FLOPS = 2 * K * H * S + 2 * H * N * S


def entries(lst, a, b):
    return lst[:, a // 16 : b // 16]


def tile_picked_hwlesapagtwo_none_p_kernel(
    tc, x_words, x_scales, d_words, d_scales, sl, th, gn, w1_words, w1_scales, offs, ci, n1, n2, n3, n4, out
):
    nc = tc.nc
    with ExitStack() as ctx:
        lists = ctx.enter_context(tc.tile_pool(name="lists", bufs=1))
        keep = ctx.enter_context(tc.tile_pool(name="keep", bufs=1))
        reuse = ctx.enter_context(tc.tile_pool(name="reuse", bufs=1))
        psum = ctx.enter_context(tc.psum_pool(name="psum", bufs=1))

        def load_list(src, name):
            tile = lists.tile([P, src.shape[1]], U16, name=name)
            nc.sync.dma_start(tile[:], src)
            return tile

        x_bytes = keep.tile([P, T], U8, name="x_bytes")
        d_bytes = keep.tile([P, T], U8, name="d_bytes")
        plane1 = keep.tile([P, S + H], U8, name="plane1", align_bytes=64)
        for tile in (x_bytes, d_bytes, plane1):
            nc.vector.memset(tile[:].bitcast(I32), 0)

        x_table = keep.tile([P, T], U32, name="x_table")
        d_table = reuse.tile([P, T], U32, name="d_table", offset=0, align_bytes=64)
        offs_t = load_list(offs, "offs_t")
        ci_t = load_list(ci, "ci_t")
        n1_t = load_list(n1, "n1_t")
        n2_t = load_list(n2, "n2_t")
        n3_t = load_list(n3, "n3_t")
        nc.sync.dma_start(x_bytes[0:P:8, :].bitcast(I32), x_scales[0].bitcast(I32))
        nc.sync.dma_start(d_bytes[0:P:8, :].bitcast(I32), d_scales[0].bitcast(I32))
        nc.sync.dma_start(d_table[:].bitcast(I32), d_words[0].rearrange("p c r -> p (c r)").bitcast(I32))
        n4_t = load_list(n4, "n4_t")
        nc.sync.dma_start(x_table[:].bitcast(I32), x_words[0].rearrange("p c r -> p (c r)").bitcast(I32))

        sl_t = keep.tile([P, PACK], F32, name="sl_t")
        th_t = keep.tile([P, PACK], F32, name="th_t")
        gn_t = keep.tile([P, PACK], F32, name="gn_t")
        for tile, src in ((sl_t, sl), (th_t, th), (gn_t, gn)):
            nc.gpsimd.dma_start(tile[:], src.rearrange("(p t) o -> p (t o)", t=PACK))

        picked_bytes = keep.tile([P, S + H], U8, name="picked_bytes")
        nc.vector.tensor_copy(picked_bytes[:, 0:S], x_bytes[:].indirect(offs_t[:]))
        nc.vector.tensor_copy(picked_bytes[:, S : S + H].rearrange("p (t m) -> p m t", t=PACK), d_bytes[:].indirect(ci_t[:]))
        for k in range(4):
            nc.scalar.dma_start(plane1[k:P:32, :].bitcast(I32), picked_bytes[8 * k : P : 32, :].bitcast(I32))

        d_codes = keep.tile([P, H], U32, name="d_codes", align_bytes=64)
        x_codes = keep.tile([P, S], U32, name="x_codes", align_bytes=64)
        nc.vector.tensor_copy(d_codes[:].rearrange("p (t m) -> p m t", t=PACK), d_table[:].indirect(ci_t[:]))
        w_codes = reuse.tile([P, 2 * N], U8, name="w_codes", offset=0, align_bytes=64)
        w_plane = reuse.tile([P, N], U8, name="w_plane", offset=2 * N, align_bytes=64)
        bias_t = reuse.tile([P, PACK], F32, name="bias_t", offset=3 * N, align_bytes=64)
        nc.vector.memset(w_plane[:].bitcast(I32), 0)
        nc.sync.dma_start(w_codes[:].bitcast(I32), w1_words[0].bitcast(I32))
        for q in range(4):
            nc.sync.dma_start(w_plane[32 * q : 32 * q + 4, :].bitcast(I32), w1_scales[0, 4 * q : 4 * q + 4, :].bitcast(I32))
        nc.vector.scalar_tensor_tensor(bias_t[:], sl_t[:], -1.0, th_t[:], ALU.mult, ALU.mult)
        nc.vector.tensor_copy(x_codes[:], x_table[:].indirect(offs_t[:]))

        s_rows = []
        for t in range(PACK):
            acc = psum.tile([P, S], F32, name="s_acc%d" % t)
            nc.tensor.matmul_mx(
                out=acc[:],
                lhsT=d_codes[:, t * P : (t + 1) * P].bitcast(FP8X4),
                lhsT_scale=plane1[:, S + t * P : S + (t + 1) * P],
                rhs=x_codes[:].bitcast(FP8X4),
                rhs_scale=plane1[:, 0:S],
                start=True,
                stop=True,
            )
            s_t = keep.tile([P, S], F32, name="s%d" % t)
            nc.vector.tensor_scalar(s_t[:], acc[:], 0.0625, None, ALU.mult)
            s_rows.append(s_t)

        h_all = keep.tile([P, N // P, S], F32, name="h_all")
        for half in range(2):
            c0, c1 = half * HALF, (half + 1) * HALF
            sg = keep.tile([P, PACK, HALF], F32, name="sg%d" % half)
            z = keep.tile([P, PACK, HALF], BF16, name="z")
            for t in range(PACK):
                nc.scalar.activation(
                    sg[:, t, :], s_rows[t][:].indirect(entries(n1_t, c0, c1)), ACT.Sigmoid,
                    bias=bias_t[:, t : t + 1], scale=sl_t[:, t : t + 1],
                )
                nc.vector.scalar_tensor_tensor(
                    z[:, t, :], s_rows[t][:, c0:c1], gn_t[:, t : t + 1], sg[:, t, :], ALU.mult, ALU.mult
                )
            z_in = keep.tile([P, HALF, PACK], BF16, name="z_in%d" % half, align_bytes=64)
            nc.vector.tensor_copy(
                z_in[:].rearrange("p (c i) t -> p c t i", i=4), z[:].rearrange("p t (c i) -> p c t i", i=4)
            )
            z_codes = keep.tile([P, HALF], U32, name="z_codes%d" % half, align_bytes=64)
            z_plane = keep.tile([P, HALF], U8, name="z_plane%d" % half, align_bytes=64)
            nc.vector.quantize_mx(z_codes[:].bitcast(FP8X4), z_plane[:], z_in[:].rearrange("p j t -> p (j t)"))
            for m0, m1 in ((0, 1), (1, 4)) if half == 0 else ((0, 4),):
                acc = psum.tile([P, m1 - m0, HALF], F32, name="h_acc%d_%d" % (half, m0))
                for m in range(m0, m1):
                    nc.tensor.matmul_mx(
                        out=acc[:, m - m0, :],
                        lhsT=w_codes[:, 2 * m * P : 2 * (m + 1) * P].bitcast(FP4X4),
                        lhsT_scale=w_plane[:, m * P : (m + 1) * P],
                        rhs=z_codes[:].bitcast(FP8X4),
                        rhs_scale=z_plane[:],
                        start=True,
                        stop=True,
                    )
                if m1 == 1:
                    nc.scalar.copy(h_all[:, m0:m1, c0:c1], acc[:])
                else:
                    nc.vector.tensor_copy(h_all[:, m0:m1, c0:c1], acc[:])

        pages = [keep.tile([P, U], F32, name="page%d" % m) for m in range(N // P)]

        def put(m, lst, factor, c0, c1):
            nc.scalar.activation(pages[m][:].indirect(entries(lst, c0, c1)), h_all[:, m, c0:c1], ACT.Copy, scale=factor)

        def take(m, w0, w1):
            other = keep.tile([P, w1 - w0], F32, name="other%d_%d" % (m, w0))
            nc.scalar.activation(other[:], pages[m][:].indirect(entries(n4_t, w0, w1)), ACT.Copy)
            res = keep.tile([P, w1 - w0], F32, name="res%d_%d" % (m, w0))
            nc.vector.tensor_tensor(res[:], pages[m][:, w0:w1], other[:], ALU.subtract)
            nc.sync.dma_start(out[m * P : (m + 1) * P, w0:w1], res[:])

        for pair in ((0, 1), (2, 3)):
            for c0, c1 in ((0, HALF), (HALF, S)) if pair[0] == 0 else ((0, S),):
                for lst, factor in ((n2_t, 1.0), (n3_t, 0.5)):
                    for m in pair:
                        put(m, lst, factor, c0, c1)
            for m in pair:
                cuts = (0, 256, 448, U) if m == N // P - 1 else (0, 256, U)
                for w0, w1 in zip(cuts, cuts[1:]):
                    take(m, w0, w1)
